import numpy as np
import ml_dtypes


def mxq(x, axis, fmt="e4m3"):
    dtype, down = {"e4m3": (ml_dtypes.float8_e4m3fn, 7), "e5m2": (ml_dtypes.float8_e5m2, 14)}[fmt]
    v = np.moveaxis(np.asarray(x, np.float32).astype(ml_dtypes.bfloat16).astype(np.float64), axis, -1)
    blocks = v.reshape(v.shape[:-1] + (-1, 32))
    amax = np.abs(blocks).max(-1, keepdims=True)
    byte = np.maximum(np.where(amax > 0, np.frexp(amax)[1] - 1 + 127, 0) - down, 1)
    scale = np.exp2(byte - 127.0)
    codes = (blocks / scale).astype(np.float32).astype(dtype).astype(np.float64)
    return np.moveaxis((codes * scale).reshape(v.shape), -1, axis)


WIDE = False


def mx_kscale(k):
    if not WIDE:
        return np.ones(k)
    levels = np.array([10, -10, 5, -5, 0])
    if k % 512:
        return np.exp2(np.random.permutation(np.resize(levels, k // 32))).repeat(32)
    a = np.empty((k // 512, 16))
    for p in range(k // 512):
        a[p, :8] = np.random.permutation(np.resize(levels, 8))
        for g in range(8):
            far = levels[np.abs(levels - a[p, g]) >= 10]
            a[p, g + 8] = far[np.random.randint(len(far))]
    return np.exp2(a.ravel()).repeat(32)


def f64(x):
    return np.asarray(x).astype(np.float64)


def striped(idx):
    return np.tile(idx.reshape(-1, 16).T, (8, 1)).astype(np.uint16)


def unstriped(offs):
    return offs[:16].T.reshape(-1).astype(np.int64)


def pack_weight(w):
    k, n = w.shape
    w = f64(np.asarray(w, np.float32).astype(ml_dtypes.bfloat16)).reshape(k // 32, 32, n)
    amax = np.abs(w).max(1)
    byte = np.clip(np.where(amax > 0, np.frexp(amax)[1] - 1 + 127 - 7, 1), 1, 254)
    scaled = (w * np.exp2(127.0 - byte)[:, None, :]).reshape(k, n).astype(np.float32)
    words = np.ascontiguousarray(scaled.reshape(k // 512, 128, 4, n).transpose(0, 1, 3, 2)).astype(ml_dtypes.float8_e4m3fn).view(np.uint8)
    return words, np.ascontiguousarray(byte.astype(np.uint8).reshape(k // 512, 16, n))


def unpack_weight(words, scales):
    g, p, n, _ = words.shape
    vals = np.ascontiguousarray(words).view(ml_dtypes.float8_e4m3fn).astype(np.float64) * np.repeat(np.exp2(scales.astype(np.float64) - 127.0), 8, axis=1)[..., None]
    return vals.transpose(0, 1, 3, 2).reshape(g * 512, n)


E2M1 = np.array([0.0, 0.5, 1.0, 1.5, 2.0, 3.0, 4.0, 6.0, -0.0, -0.5, -1.0, -1.5, -2.0, -3.0, -4.0, -6.0])


def pack_fp4(w):
    k, n = w.shape
    w = f64(np.asarray(w, np.float32).astype(ml_dtypes.bfloat16)).reshape(k // 32, 32, n)
    amax = np.abs(w).max(1)
    mant, ex = np.frexp(amax / 6.0)
    byte = np.clip(np.where(amax > 0, np.where(mant > 0.5, ex, ex - 1) + 127, 1), 1, 254)
    scaled = (w * np.exp2(127.0 - byte)[:, None, :]).reshape(k, n).astype(np.float32)
    c = np.ascontiguousarray(scaled.reshape(k // 512, 128, 4, n).transpose(0, 1, 3, 2)).astype(ml_dtypes.float4_e2m1fn).view(np.uint8) & 0xF
    words = (c[..., 0::2] | (c[..., 1::2] << 4)).reshape(k // 512, 128, 2 * n)
    return np.ascontiguousarray(words), np.ascontiguousarray(byte.astype(np.uint8).reshape(k // 512, 16, n))


def unpack_fp4(words, scales):
    g, _, n = scales.shape
    words = np.ascontiguousarray(words).reshape(g, 128, n, 2)
    nib = np.empty((g, 128, n, 4), np.uint8)
    nib[..., 0::2] = words & 0xF
    nib[..., 1::2] = words >> 4
    vals = E2M1[nib] * np.repeat(np.exp2(scales.astype(np.float64) - 127.0), 8, axis=1)[..., None]
    return vals.transpose(0, 1, 3, 2).reshape(g * 512, n)


def planes(y):
    n, m = y.shape
    v = y.astype(np.float32).astype(ml_dtypes.bfloat16).astype(np.float64).reshape(n // 32, 32, m)
    top = np.abs(v).max(1)
    byte = np.clip(np.where(top > 0, np.frexp(top)[1] - 1 + 127 - 7, 1), 1, 254)
    codes = (v * np.exp2(127.0 - byte)[:, None, :]).reshape(n, m).astype(np.float32).astype(ml_dtypes.float8_e4m3fn).view(np.uint8)
    words = codes.reshape(n // 512, 128, 4, m).transpose(0, 1, 3, 2)
    return np.ascontiguousarray(words), np.ascontiguousarray(byte.astype(np.uint8).reshape(n // 512, 16, m))


K, T, S, N, H, U = 512, 2048, 512, 512, 512, 1024


def setup_inputs():
    n = np.random.standard_normal
    s = mx_kscale(K)[:, None]
    u = mx_kscale(H)
    packed_xT = pack_weight(n((K, T)) * s)
    packed_w1 = pack_fp4(n((K, N)) / np.sqrt(K) / s)
    packed_w3 = pack_fp4(n((H, N)) / np.sqrt(H) / u[:, None])
    return {
        "x_words": packed_xT[0],
        "x_scales": packed_xT[1],
        "w1_words": packed_w1[0],
        "w1_scales": packed_w1[1],
        "unit": (np.random.uniform(0.6, 1.4, (H, 1)) * u[:, None]).astype(np.float32),
        "w3_words": packed_w3[0],
        "w3_scales": packed_w3[1],
        "offs": striped(np.random.permutation(T)[:S]),
        "lef": striped(np.random.permutation(np.concatenate([np.arange(S), np.random.randint(0, S, U - S)]))),
        "rig": striped(np.random.permutation(np.concatenate([np.arange(S), np.random.randint(0, S, U - S)]))),
        "mid": striped(np.random.permutation(np.concatenate([np.arange(S), np.random.randint(0, S, U - S)]))),
    }


def reference(x_words, x_scales, w1_words, w1_scales, unit, w3_words, w3_scales, offs, lef, rig, mid):
    xq = unpack_weight(x_words, x_scales)[:, unstriped(offs)]
    y = unpack_fp4(w1_words, w1_scales).T @ xq
    ym = y[:, unstriped(mid)]
    yl = y[:, unstriped(lef)]
    yr = y[:, unstriped(rig)]
    ends = yl + yr
    hid = f64(unit) * (ym - (0.5 * ends))
    out_0 = unpack_fp4(w3_words, w3_scales).T @ mxq(hid, 0, "e4m3")
    return (out_0,) + planes(out_0)

@@ -1,0 +1,195 @@
+from contextlib import ExitStack
+
+import concourse.mybir as mybir
+
+K, T, S, N, H, U = 512, 2048, 512, 512, 512, 1024
+FLOPS = 2 * K * N * S + 2 * H * N * U
+
+F32 = mybir.dt.float32
+BF16 = mybir.dt.bfloat16
+I32 = mybir.dt.int32
+U32 = mybir.dt.uint32
+U16 = mybir.dt.uint16
+U8 = mybir.dt.uint8
+FP8X4 = mybir.dt.float8_e4m3fn_x4
+FP4X4 = mybir.dt.float4_e2m1fn_x4
+COPY = mybir.ActivationFunctionType.Copy
+ADD = mybir.AluOpType.add
+MULT = mybir.AluOpType.mult
+
+P = 128
+PACK = 4
+BANK = 512
+LIST = 16
+CHUNKS = ((0, 256, 192), (256, 256, 192), (512, 256, 192), (768, 128, 64), (896, 128, 128))
+
+
+def load_scale_rows(queue, tile, rows):
+    for q in range(4):
+        queue.dma_start(out=tile[32 * q : 32 * q + 4, :].bitcast(I32), in_=rows[0, 4 * q : 4 * q + 4, :].bitcast(I32))
+
+
+def deal(nc, words, scales, raw_words, raw_scales):
+    nc.vector.tensor_copy(
+        out=words[:].rearrange("p (t m b) -> p t m b", t=PACK, b=2),
+        in_=raw_words[:].rearrange("p (m t b) -> p t m b", t=PACK, b=2),
+    )
+    nc.vector.tensor_copy(
+        out=scales[:].rearrange("p (t m) -> p t m", t=PACK),
+        in_=raw_scales[:].rearrange("p (m t) -> p t m", t=PACK),
+    )
+
+
+def planes_view(ap):
+    return ap.rearrange("p t (c i) -> p c t i", i=2)
+
+
+def packed_view(ap):
+    return ap.rearrange("p (c i) t -> p c t i", i=2)
+
+
+def tile_picked_ybrdgep_sag_po_kernel(
+    tc, x_words, x_scales, w1_words, w1_scales, unit, w3_words, w3_scales, offs, lef, rig, mid, out_0, out_1, out_2
+):
+    nc = tc.nc
+    with ExitStack() as ctx:
+        keep = ctx.enter_context(tc.tile_pool(name="keep", bufs=1))
+        psum = ctx.enter_context(tc.psum_pool(name="psum", bufs=1))
+
+        offs_t = keep.tile([P, S // LIST], U16, name="offs_t")
+        mid_t = keep.tile([P, U // LIST], U16, name="mid_t")
+        lef_t = keep.tile([P, U // LIST], U16, name="lef_t")
+        rig_t = keep.tile([P, U // LIST], U16, name="rig_t")
+        x_all = keep.tile([P, T], I32, name="x_all", align_bytes=64)
+        xs_all = keep.tile([P, T], U8, name="xs_all", align_bytes=64)
+        w1_raw = keep.tile([P, 2 * N], U8, name="w1_raw", align_bytes=64)
+        w1s_raw = keep.tile([P, N], U8, name="w1s_raw", align_bytes=64)
+        w3_raw = keep.tile([P, 2 * N], U8, name="w3_raw", align_bytes=64)
+        w3s_raw = keep.tile([P, N], U8, name="w3s_raw", align_bytes=64)
+        unit_t = keep.tile([P, PACK], F32, name="unit_t")
+
+        nc.vector.memset(xs_all[:].bitcast(I32), 0)
+        nc.gpsimd.memset(w1s_raw[:].bitcast(I32), 0)
+        nc.gpsimd.memset(w3s_raw[:].bitcast(I32), 0)
+
+        x_flat = x_words[0].rearrange("p n t -> p (n t)").bitcast(I32)
+        nc.sync.dma_start(offs_t[:], offs)
+        nc.sync.dma_start(out=w1_raw[:].bitcast(I32), in_=w1_words[0].bitcast(I32))
+        nc.sync.dma_start(out=x_all[:, : T // 2], in_=x_flat[:, : T // 2])
+        load_scale_rows(nc.sync, xs_all, x_scales)
+        nc.sync.dma_start(out=x_all[:, T // 2 :], in_=x_flat[:, T // 2 :])
+        load_scale_rows(nc.scalar, w1s_raw, w1_scales)
+        nc.scalar.dma_start(out=unit_t[:], in_=unit.rearrange("(p t) o -> p (t o)", t=PACK))
+        nc.sync.dma_start(mid_t[:], mid)
+        nc.sync.dma_start(rig_t[:], rig)
+        nc.sync.dma_start(lef_t[:], lef)
+        nc.sync.dma_start(out=w3_raw[:].bitcast(I32), in_=w3_words[0].bitcast(I32))
+        load_scale_rows(nc.sync, w3s_raw, w3_scales)
+
+        w1_t = keep.tile([P, 2 * N], U8, name="w1_t", align_bytes=64)
+        w1s_t = keep.tile([P, N], U8, name="w1s_t", align_bytes=64)
+        w3_t = keep.tile([P, 2 * N], U8, name="w3_t", align_bytes=64)
+        w3s_t = keep.tile([P, N], U8, name="w3s_t", align_bytes=64)
+        deal(nc, w1_t, w1s_t, w1_raw, w1s_raw)
+
+        half = keep.tile([P, PACK], F32, name="half")
+        nc.scalar.activation(half[:], unit_t[:], COPY, scale=-0.5)
+
+        xs_picked = keep.tile([P, S], U8, name="xs_picked", align_bytes=64)
+        x_picked = keep.tile([P, S], U32, name="x_picked", align_bytes=64)
+        nc.vector.tensor_copy(xs_picked[:], xs_all[:].indirect(offs_t[:]))
+        nc.vector.tensor_copy(x_picked[:], x_all[:].bitcast(U32).indirect(offs_t[:]))
+
+        windows = []
+        for t in range(PACK):
+            acc = psum.tile([P, S], F32, name="y%d" % t)
+            nc.tensor.matmul_mx(
+                out=acc[:],
+                lhsT=w1_t[:, 2 * P * t : 2 * P * (t + 1)].bitcast(FP4X4),
+                lhsT_scale=w1s_t[:, P * t : P * (t + 1)],
+                rhs=x_picked[:].bitcast(FP8X4),
+                rhs_scale=xs_picked[:],
+                start=True,
+                stop=True,
+            )
+            window = keep.tile([P, S], F32, name="window%d" % t, align_bytes=64)
+            if t == 0:
+                nc.scalar.activation(window[:], acc[:], COPY, scale=half[:, t : t + 1])
+            else:
+                nc.vector.tensor_scalar(window[:], acc[:], half[:, t : t + 1], None, MULT)
+            windows.append(window)
+        deal(nc, w3_t, w3s_t, w3_raw, w3s_raw)
+
+        out_rows = out_0.rearrange("(p t) r -> p t r", t=PACK)
+        out_words = out_1[0].rearrange("p n t -> p (n t)").bitcast(I32)
+        out_scales = keep.tile([P, U], U8, name="out_scales", align_bytes=64)
+
+        def entries(tile, first, count):
+            return tile[:, first // LIST : (first + count) // LIST]
+
+        def look_up(n):
+            r0, width, shared = CHUNKS[n]
+            middle = keep.tile([P, PACK, width], F32, name="middle%d" % n, align_bytes=64)
+            left = keep.tile([P, PACK, shared], F32, name="left%d" % n, align_bytes=64)
+            part = keep.tile([P, PACK, width], F32, name="part%d" % n, align_bytes=64)
+            hid = keep.tile([P, width, PACK], BF16, name="hid%d" % n, align_bytes=64)
+            for t in range(PACK):
+                nc.scalar.activation(middle[:, t, :], windows[t][:].indirect(entries(mid_t, r0, width)), COPY, scale=-2.0)
+                nc.vector.tensor_tensor(part[:, t, :], windows[t][:].indirect(entries(rig_t, r0, width)), middle[:, t, :], ADD)
+            for t in range(PACK):
+                nc.scalar.activation(left[:, t, :], windows[t][:].indirect(entries(lef_t, r0, shared)), COPY)
+            rest = width - shared
+            if rest:
+                whole = keep.tile([P, PACK, rest], F32, name="whole%d" % n, align_bytes=64)
+                for t in range(PACK):
+                    nc.vector.tensor_tensor(
+                        whole[:, t, :], windows[t][:].indirect(entries(lef_t, r0 + shared, rest)), part[:, t, shared:], ADD
+                    )
+                nc.vector.tensor_copy(out=packed_view(hid[:, shared:, :]), in_=planes_view(whole[:]))
+            nc.vector.tensor_tensor(packed_view(hid[:, :shared, :]), planes_view(part[:, :, :shared]), planes_view(left[:]), ADD)
+            return hid
+
+        def multiply(n, hid):
+            r0, width, shared = CHUNKS[n]
+            codes = keep.tile([P, width], U32, name="hid_codes%d" % n, align_bytes=64)
+            scales = keep.tile([P, width], U8, name="hid_scales%d" % n, align_bytes=64)
+            nc.vector.quantize_mx(out=codes[:].bitcast(FP8X4), scales=scales[:], in_=hid[:].rearrange("p r t -> p (r t)"))
+            result = keep.tile([P, PACK, width], F32, name="result%d" % n, align_bytes=64)
+            for pair in range(2):
+                acc = psum.tile([P, 2, width], F32, name="o%d" % (2 * (n % 2) + pair))
+                for e in range(2):
+                    t = 2 * pair + e
+                    nc.tensor.matmul_mx(
+                        out=acc[:, e, :],
+                        lhsT=w3_t[:, 2 * P * t : 2 * P * (t + 1)].bitcast(FP4X4),
+                        lhsT_scale=w3s_t[:, P * t : P * (t + 1)],
+                        rhs=codes[:].bitcast(FP8X4),
+                        rhs_scale=scales[:],
+                        start=True,
+                        stop=True,
+                    )
+                nc.scalar.copy(result[:, 2 * pair : 2 * pair + 2, :], acc[:])
+            nc.sync.dma_start(out=out_rows[:, :, r0 : r0 + width], in_=result[:])
+            return result
+
+        def hand_on(n, result):
+            r0, width, shared = CHUNKS[n]
+            rounded = keep.tile([P, width, PACK], BF16, name="rounded%d" % n, align_bytes=64)
+            nc.vector.tensor_copy(out=packed_view(rounded[:]), in_=planes_view(result[:]))
+            codes = keep.tile([P, width], I32, name="out_codes%d" % n, align_bytes=64)
+            nc.vector.quantize_mx(
+                out=codes[:].bitcast(FP8X4), scales=out_scales[:, r0 : r0 + width], in_=rounded[:].rearrange("p r t -> p (r t)")
+            )
+            nc.sync.dma_start(out=out_words[:, r0 : r0 + width], in_=codes[:])
+
+        hids, results = {}, {}
+        for n in range(len(CHUNKS) + 2):
+            if n < len(CHUNKS):
+                hids[n] = look_up(n)
+            if 0 <= n - 1 < len(CHUNKS):
+                results[n - 1] = multiply(n - 1, hids[n - 1])
+            if 0 <= n - 2:
+                hand_on(n - 2, results[n - 2])
+        for q in range(4):
+            queue = nc.sync if q % 2 == 0 else nc.scalar
+            queue.dma_start(out=out_2[0, 4 * q : 4 * q + 4, :].bitcast(I32), in_=out_scales[32 * q : 32 * q + 4, :].bitcast(I32))

@@ -21,23 +21,30 @@ P = 128
 PACK = 4
 BANK = 512
 LIST = 16
-CHUNKS = ((0, 256, 192), (256, 256, 192), (512, 256, 192), (768, 128, 64), (896, 128, 128))
+CHUNKS = ((0, 256, 128), (256, 384, 128), (640, 256, 256), (896, 128, 128))
 
 
-def load_scale_rows(queue, tile, rows):
+def load_scale_rows(queues, tile, rows):
     for q in range(4):
-        queue.dma_start(out=tile[32 * q : 32 * q + 4, :].bitcast(I32), in_=rows[0, 4 * q : 4 * q + 4, :].bitcast(I32))
+        queues[q].dma_start(out=tile[32 * q : 32 * q + 4, :].bitcast(I32), in_=rows[0, 4 * q : 4 * q + 4, :].bitcast(I32))
 
 
-def deal(nc, words, scales, raw_words, raw_scales):
+def deal_words(nc, words, raw):
     nc.vector.tensor_copy(
         out=words[:].rearrange("p (t m b) -> p t m b", t=PACK, b=2),
-        in_=raw_words[:].rearrange("p (m t b) -> p t m b", t=PACK, b=2),
+        in_=raw[:].rearrange("p (m t b) -> p t m b", t=PACK, b=2),
     )
+
+
+def deal_scales(nc, scales, raw):
     nc.vector.tensor_copy(
         out=scales[:].rearrange("p (t m) -> p t m", t=PACK),
-        in_=raw_scales[:].rearrange("p (m t) -> p t m", t=PACK),
+        in_=raw[:].rearrange("p (m t) -> p t m", t=PACK),
     )
+
+
+def entries(tile, first, count):
+    return tile[:, first // LIST : (first + count) // LIST]
 
 
 def planes_view(ap):
@@ -69,75 +76,73 @@ def tile_picked_ybrdgep_sag_po_kernel(
         unit_t = keep.tile([P, PACK], F32, name="unit_t")
 
         nc.vector.memset(xs_all[:].bitcast(I32), 0)
-        nc.gpsimd.memset(w1s_raw[:].bitcast(I32), 0)
-        nc.gpsimd.memset(w3s_raw[:].bitcast(I32), 0)
+        nc.vector.memset(w1s_raw[:].bitcast(I32), 0)
+        nc.vector.memset(w3s_raw[:].bitcast(I32), 0)
 
         x_flat = x_words[0].rearrange("p n t -> p (n t)").bitcast(I32)
         nc.sync.dma_start(offs_t[:], offs)
         nc.sync.dma_start(out=w1_raw[:].bitcast(I32), in_=w1_words[0].bitcast(I32))
-        nc.sync.dma_start(out=x_all[:, : T // 2], in_=x_flat[:, : T // 2])
-        load_scale_rows(nc.sync, xs_all, x_scales)
-        nc.sync.dma_start(out=x_all[:, T // 2 :], in_=x_flat[:, T // 2 :])
-        load_scale_rows(nc.scalar, w1s_raw, w1_scales)
-        nc.scalar.dma_start(out=unit_t[:], in_=unit.rearrange("(p t) o -> p (t o)", t=PACK))
+        load_scale_rows((nc.sync, nc.scalar, nc.sync, nc.scalar), xs_all, x_scales)
+        nc.sync.dma_start(out=x_all[:], in_=x_flat)
+        load_scale_rows((nc.sync,) * 4, w1s_raw, w1_scales)
+        nc.sync.dma_start(out=unit_t[:], in_=unit.rearrange("(p t) o -> p (t o)", t=PACK))
         nc.sync.dma_start(mid_t[:], mid)
         nc.sync.dma_start(rig_t[:], rig)
         nc.sync.dma_start(lef_t[:], lef)
         nc.sync.dma_start(out=w3_raw[:].bitcast(I32), in_=w3_words[0].bitcast(I32))
-        load_scale_rows(nc.sync, w3s_raw, w3_scales)
+        load_scale_rows((nc.sync,) * 4, w3s_raw, w3_scales)
 
         w1_t = keep.tile([P, 2 * N], U8, name="w1_t", align_bytes=64)
         w1s_t = keep.tile([P, N], U8, name="w1s_t", align_bytes=64)
         w3_t = keep.tile([P, 2 * N], U8, name="w3_t", align_bytes=64)
         w3s_t = keep.tile([P, N], U8, name="w3s_t", align_bytes=64)
-        deal(nc, w1_t, w1s_t, w1_raw, w1s_raw)
 
         half = keep.tile([P, PACK], F32, name="half")
         nc.scalar.activation(half[:], unit_t[:], COPY, scale=-0.5)
 
         xs_picked = keep.tile([P, S], U8, name="xs_picked", align_bytes=64)
-        x_picked = keep.tile([P, S], U32, name="x_picked", align_bytes=64)
         nc.vector.tensor_copy(xs_picked[:], xs_all[:].indirect(offs_t[:]))
-        nc.vector.tensor_copy(x_picked[:], x_all[:].bitcast(U32).indirect(offs_t[:]))
-
-        windows = []
+        deal_words(nc, w1_t, w1_raw)
+        windows = [keep.tile([P, S], F32, name="window%d" % t, align_bytes=64) for t in range(PACK)]
+        x_picked = [keep.tile([P, S // 2], U32, name="x_picked%d" % h, align_bytes=64) for h in range(2)]
+        nc.vector.tensor_copy(x_picked[0][:], x_all[:].bitcast(U32).indirect(entries(offs_t, 0, S // 2)))
+        deal_scales(nc, w1s_t, w1s_raw)
+        nc.vector.tensor_copy(x_picked[1][:], x_all[:].bitcast(U32).indirect(entries(offs_t, S // 2, S // 2)))
         for t in range(PACK):
-            acc = psum.tile([P, S], F32, name="y%d" % t)
-            nc.tensor.matmul_mx(
-                out=acc[:],
-                lhsT=w1_t[:, 2 * P * t : 2 * P * (t + 1)].bitcast(FP4X4),
-                lhsT_scale=w1s_t[:, P * t : P * (t + 1)],
-                rhs=x_picked[:].bitcast(FP8X4),
-                rhs_scale=xs_picked[:],
-                start=True,
-                stop=True,
-            )
-            window = keep.tile([P, S], F32, name="window%d" % t, align_bytes=64)
-            if t == 0:
-                nc.scalar.activation(window[:], acc[:], COPY, scale=half[:, t : t + 1])
-            else:
-                nc.vector.tensor_scalar(window[:], acc[:], half[:, t : t + 1], None, MULT)
-            windows.append(window)
-        deal(nc, w3_t, w3s_t, w3_raw, w3s_raw)
+            for h in range(2):
+                acc = psum.tile([P, S // 2], F32, name="bank%d" % (2 * t + h))
+                nc.tensor.matmul_mx(
+                    out=acc[:],
+                    lhsT=w1_t[:, 2 * P * t : 2 * P * (t + 1)].bitcast(FP4X4),
+                    lhsT_scale=w1s_t[:, P * t : P * (t + 1)],
+                    rhs=x_picked[h][:].bitcast(FP8X4),
+                    rhs_scale=xs_picked[:, h * S // 2 : (h + 1) * S // 2],
+                    start=True,
+                    stop=True,
+                )
+                columns = windows[t][:, h * S // 2 : (h + 1) * S // 2]
+                if t in (0, 3):
+                    nc.scalar.activation(columns, acc[:], COPY, scale=half[:, t : t + 1])
+                else:
+                    nc.vector.tensor_scalar(columns, acc[:], half[:, t : t + 1], None, MULT)
+        deal_words(nc, w3_t, w3_raw)
+        deal_scales(nc, w3s_t, w3s_raw)
 
         out_rows = out_0.rearrange("(p t) r -> p t r", t=PACK)
         out_words = out_1[0].rearrange("p n t -> p (n t)").bitcast(I32)
         out_scales = keep.tile([P, U], U8, name="out_scales", align_bytes=64)
 
-        def entries(tile, first, count):
-            return tile[:, first // LIST : (first + count) // LIST]
-
         def look_up(n):
             r0, width, shared = CHUNKS[n]
-            middle = keep.tile([P, PACK, width], F32, name="middle%d" % n, align_bytes=64)
+            middle = keep.tile([P, PACK, width], F32, name="stage%d" % (n % 2), align_bytes=64)
             left = keep.tile([P, PACK, shared], F32, name="left%d" % n, align_bytes=64)
             part = keep.tile([P, PACK, width], F32, name="part%d" % n, align_bytes=64)
-            hid = keep.tile([P, width, PACK], BF16, name="hid%d" % n, align_bytes=64)
             for t in range(PACK):
                 nc.scalar.activation(middle[:, t, :], windows[t][:].indirect(entries(mid_t, r0, width)), COPY, scale=-2.0)
                 nc.vector.tensor_tensor(part[:, t, :], windows[t][:].indirect(entries(rig_t, r0, width)), middle[:, t, :], ADD)
             for t in range(PACK):
                 nc.scalar.activation(left[:, t, :], windows[t][:].indirect(entries(lef_t, r0, shared)), COPY)
+            hid = keep.tile([P, width, PACK], BF16, name="stage%d" % (n % 2), align_bytes=64)
             rest = width - shared
             if rest:
                 whole = keep.tile([P, PACK, rest], F32, name="whole%d" % n, align_bytes=64)
@@ -145,51 +150,80 @@ def tile_picked_ybrdgep_sag_po_kernel(
                     nc.vector.tensor_tensor(
                         whole[:, t, :], windows[t][:].indirect(entries(lef_t, r0 + shared, rest)), part[:, t, shared:], ADD
                     )
-                nc.vector.tensor_copy(out=packed_view(hid[:, shared:, :]), in_=planes_view(whole[:]))
-            nc.vector.tensor_tensor(packed_view(hid[:, :shared, :]), planes_view(part[:, :, :shared]), planes_view(left[:]), ADD)
-            return hid
+            else:
+                whole = None
+            return hid, part, left, whole
 
-        def multiply(n, hid):
+        def round_rest(n, hid, part, left, whole):
             r0, width, shared = CHUNKS[n]
+            if shared < width:
+                nc.vector.tensor_copy(out=packed_view(hid[:, shared:, :]), in_=planes_view(whole[:]))
+
+        def multiply(n, hid, part, left, whole):
+            r0, width, shared = CHUNKS[n]
+            nc.vector.tensor_tensor(packed_view(hid[:, :shared, :]), planes_view(part[:, :, :shared]), planes_view(left[:]), ADD)
             codes = keep.tile([P, width], U32, name="hid_codes%d" % n, align_bytes=64)
             scales = keep.tile([P, width], U8, name="hid_scales%d" % n, align_bytes=64)
             nc.vector.quantize_mx(out=codes[:].bitcast(FP8X4), scales=scales[:], in_=hid[:].rearrange("p r t -> p (r t)"))
+            banks = []
+            last = n == len(CHUNKS) - 1
+            for block in range(width // P):
+                for first, count in ((0, 2), (2, 2)) if last else ((0, PACK),):
+                    acc = psum.tile([P, count, P], F32, name="bank%d" % ((r0 // P + block + first // 2) % 8))
+                    for t in range(first, first + count):
+                        nc.tensor.matmul_mx(
+                            out=acc[:, t - first, :],
+                            lhsT=w3_t[:, 2 * P * t : 2 * P * (t + 1)].bitcast(FP4X4),
+                            lhsT_scale=w3s_t[:, P * t : P * (t + 1)],
+                            rhs=codes[:, P * block : P * (block + 1)].bitcast(FP8X4),
+                            rhs_scale=scales[:, P * block : P * (block + 1)],
+                            start=True,
+                            stop=True,
+                        )
+                    banks.append(acc)
+            return banks
+
+        def take_out(n, banks):
+            r0, width, shared = CHUNKS[n]
             result = keep.tile([P, PACK, width], F32, name="result%d" % n, align_bytes=64)
-            for pair in range(2):
-                acc = psum.tile([P, 2, width], F32, name="o%d" % (2 * (n % 2) + pair))
-                for e in range(2):
-                    t = 2 * pair + e
-                    nc.tensor.matmul_mx(
-                        out=acc[:, e, :],
-                        lhsT=w3_t[:, 2 * P * t : 2 * P * (t + 1)].bitcast(FP4X4),
-                        lhsT_scale=w3s_t[:, P * t : P * (t + 1)],
-                        rhs=codes[:].bitcast(FP8X4),
-                        rhs_scale=scales[:],
-                        start=True,
-                        stop=True,
-                    )
-                nc.scalar.copy(result[:, 2 * pair : 2 * pair + 2, :], acc[:])
+            if n == len(CHUNKS) - 1:
+                nc.scalar.copy(result[:, 0:2, :], banks[0][:])
+                nc.vector.tensor_copy(result[:, 2:4, :], banks[1][:])
+            else:
+                for block, acc in enumerate(banks):
+                    nc.scalar.copy(result[:, :, P * block : P * (block + 1)], acc[:])
             nc.sync.dma_start(out=out_rows[:, :, r0 : r0 + width], in_=result[:])
             return result
 
-        def hand_on(n, result):
+        def round_out(n, result):
             r0, width, shared = CHUNKS[n]
             rounded = keep.tile([P, width, PACK], BF16, name="rounded%d" % n, align_bytes=64)
             nc.vector.tensor_copy(out=packed_view(rounded[:]), in_=planes_view(result[:]))
+            return rounded
+
+        def hand_on(n, rounded):
+            r0, width, shared = CHUNKS[n]
             codes = keep.tile([P, width], I32, name="out_codes%d" % n, align_bytes=64)
             nc.vector.quantize_mx(
                 out=codes[:].bitcast(FP8X4), scales=out_scales[:, r0 : r0 + width], in_=rounded[:].rearrange("p r t -> p (r t)")
             )
-            nc.sync.dma_start(out=out_words[:, r0 : r0 + width], in_=codes[:])
+            queue = nc.scalar if n == len(CHUNKS) - 1 else nc.sync
+            queue.dma_start(out=out_words[:, r0 : r0 + width], in_=codes[:])
 
-        hids, results = {}, {}
+        banks, results = {}, {}
         for n in range(len(CHUNKS) + 2):
             if n < len(CHUNKS):
-                hids[n] = look_up(n)
+                staged = look_up(n)
             if 0 <= n - 1 < len(CHUNKS):
-                results[n - 1] = multiply(n - 1, hids[n - 1])
+                results[n - 1] = take_out(n - 1, banks[n - 1])
             if 0 <= n - 2:
-                hand_on(n - 2, results[n - 2])
+                rounded = round_out(n - 2, results[n - 2])
+            if n < len(CHUNKS):
+                round_rest(n, *staged)
+            if 0 <= n - 2:
+                hand_on(n - 2, rounded)
+            if n < len(CHUNKS):
+                banks[n] = multiply(n, *staged)
         for q in range(4):
             queue = nc.sync if q % 2 == 0 else nc.scalar
             queue.dma_start(out=out_2[0, 4 * q : 4 * q + 4, :].bitcast(I32), in_=out_scales[32 * q : 32 * q + 4, :].bitcast(I32))

@@ -21,7 +21,7 @@ P = 128
 PACK = 4
 BANK = 512
 LIST = 16
-CHUNKS = ((0, 256, 128), (256, 384, 128), (640, 256, 256), (896, 128, 128))
+CHUNKS = ((0, 128, 0), (128, 384, 128), (512, 384, 384), (896, 128, 128))
 
 
 def load_scale_rows(queues, tile, rows):
@@ -84,12 +84,12 @@ def tile_picked_ybrdgep_sag_po_kernel(
         nc.sync.dma_start(out=w1_raw[:].bitcast(I32), in_=w1_words[0].bitcast(I32))
         load_scale_rows((nc.sync, nc.scalar, nc.sync, nc.scalar), xs_all, x_scales)
         nc.sync.dma_start(out=x_all[:], in_=x_flat)
-        load_scale_rows((nc.sync,) * 4, w1s_raw, w1_scales)
+        load_scale_rows((nc.scalar,) * 4, w1s_raw, w1_scales)
         nc.sync.dma_start(out=unit_t[:], in_=unit.rearrange("(p t) o -> p (t o)", t=PACK))
         nc.sync.dma_start(mid_t[:], mid)
+        nc.sync.dma_start(out=w3_raw[:].bitcast(I32), in_=w3_words[0].bitcast(I32))
         nc.sync.dma_start(rig_t[:], rig)
         nc.sync.dma_start(lef_t[:], lef)
-        nc.sync.dma_start(out=w3_raw[:].bitcast(I32), in_=w3_words[0].bitcast(I32))
         load_scale_rows((nc.sync,) * 4, w3s_raw, w3_scales)
 
         w1_t = keep.tile([P, 2 * N], U8, name="w1_t", align_bytes=64)
@@ -121,7 +121,7 @@ def tile_picked_ybrdgep_sag_po_kernel(
                     stop=True,
                 )
                 columns = windows[t][:, h * S // 2 : (h + 1) * S // 2]
-                if t in (0, 3):
+                if t % 2 == 0:
                     nc.scalar.activation(columns, acc[:], COPY, scale=half[:, t : t + 1])
                 else:
                     nc.vector.tensor_scalar(columns, acc[:], half[:, t : t + 1], None, MULT)
@@ -135,12 +135,12 @@ def tile_picked_ybrdgep_sag_po_kernel(
         def look_up(n):
             r0, width, shared = CHUNKS[n]
             middle = keep.tile([P, PACK, width], F32, name="stage%d" % (n % 2), align_bytes=64)
-            left = keep.tile([P, PACK, shared], F32, name="left%d" % n, align_bytes=64)
+            left = keep.tile([P, PACK, shared], F32, name="left%d" % n, align_bytes=64) if shared else None
             part = keep.tile([P, PACK, width], F32, name="part%d" % n, align_bytes=64)
             for t in range(PACK):
                 nc.scalar.activation(middle[:, t, :], windows[t][:].indirect(entries(mid_t, r0, width)), COPY, scale=-2.0)
                 nc.vector.tensor_tensor(part[:, t, :], windows[t][:].indirect(entries(rig_t, r0, width)), middle[:, t, :], ADD)
-            for t in range(PACK):
+            for t in range(PACK if shared else 0):
                 nc.scalar.activation(left[:, t, :], windows[t][:].indirect(entries(lef_t, r0, shared)), COPY)
             hid = keep.tile([P, width, PACK], BF16, name="stage%d" % (n % 2), align_bytes=64)
             rest = width - shared
@@ -161,7 +161,8 @@ def tile_picked_ybrdgep_sag_po_kernel(
 
         def multiply(n, hid, part, left, whole):
             r0, width, shared = CHUNKS[n]
-            nc.vector.tensor_tensor(packed_view(hid[:, :shared, :]), planes_view(part[:, :, :shared]), planes_view(left[:]), ADD)
+            if shared:
+                nc.vector.tensor_tensor(packed_view(hid[:, :shared, :]), planes_view(part[:, :, :shared]), planes_view(left[:]), ADD)
             codes = keep.tile([P, width], U32, name="hid_codes%d" % n, align_bytes=64)
             scales = keep.tile([P, width], U8, name="hid_scales%d" % n, align_bytes=64)
             nc.vector.quantize_mx(out=codes[:].bitcast(FP8X4), scales=scales[:], in_=hid[:].rearrange("p r t -> p (r t)"))
@@ -189,10 +190,12 @@ def tile_picked_ybrdgep_sag_po_kernel(
             if n == len(CHUNKS) - 1:
                 nc.scalar.copy(result[:, 0:2, :], banks[0][:])
                 nc.vector.tensor_copy(result[:, 2:4, :], banks[1][:])
+                nc.sync.dma_start(out=out_rows[:, :, r0 : r0 + width], in_=result[:])
             else:
                 for block, acc in enumerate(banks):
-                    nc.scalar.copy(result[:, :, P * block : P * (block + 1)], acc[:])
-            nc.sync.dma_start(out=out_rows[:, :, r0 : r0 + width], in_=result[:])
+                    columns = result[:, :, P * block : P * (block + 1)]
+                    nc.scalar.copy(columns, acc[:])
+                    nc.sync.dma_start(out=out_rows[:, :, r0 + P * block : r0 + P * (block + 1)], in_=columns)
             return result
 
         def round_out(n, result):

@@ -70,7 +70,7 @@ def tile_picked_ybrdgep_sag_po_kernel(
         x_all = keep.tile([P, T], I32, name="x_all", align_bytes=64)
         xs_all = keep.tile([P, T], U8, name="xs_all", align_bytes=64)
         w1_raw = keep.tile([P, 2 * N], U8, name="w1_raw", align_bytes=64)
-        w1s_raw = keep.tile([P, N], U8, name="w1s_raw", align_bytes=64)
+        w1s_raw = keep.tile([P, N], U8, name="w1s_raw", tag="handed", align_bytes=64)
         w3_raw = keep.tile([P, 2 * N], U8, name="w3_raw", align_bytes=64)
         w3s_raw = keep.tile([P, N], U8, name="w3s_raw", align_bytes=64)
         unit_t = keep.tile([P, PACK], F32, name="unit_t")
@@ -84,9 +84,9 @@ def tile_picked_ybrdgep_sag_po_kernel(
         nc.sync.dma_start(out=w1_raw[:].bitcast(I32), in_=w1_words[0].bitcast(I32))
         load_scale_rows((nc.sync, nc.scalar, nc.sync, nc.scalar), xs_all, x_scales)
         nc.sync.dma_start(out=x_all[:], in_=x_flat)
-        load_scale_rows((nc.scalar,) * 4, w1s_raw, w1_scales)
         nc.sync.dma_start(out=unit_t[:], in_=unit.rearrange("(p t) o -> p (t o)", t=PACK))
         nc.sync.dma_start(mid_t[:], mid)
+        load_scale_rows((nc.sync,) * 4, w1s_raw, w1_scales)
         nc.sync.dma_start(out=w3_raw[:].bitcast(I32), in_=w3_words[0].bitcast(I32))
         nc.sync.dma_start(rig_t[:], rig)
         nc.sync.dma_start(lef_t[:], lef)
@@ -104,9 +104,10 @@ def tile_picked_ybrdgep_sag_po_kernel(
         nc.vector.tensor_copy(xs_picked[:], xs_all[:].indirect(offs_t[:]))
         deal_words(nc, w1_t, w1_raw)
         windows = [keep.tile([P, S], F32, name="window%d" % t, align_bytes=64) for t in range(PACK)]
-        x_picked = [keep.tile([P, S // 2], U32, name="x_picked%d" % h, align_bytes=64) for h in range(2)]
+        x_picked = [keep.tile([P, S // 2], U32, name="x_picked0", align_bytes=64)]
         nc.vector.tensor_copy(x_picked[0][:], x_all[:].bitcast(U32).indirect(entries(offs_t, 0, S // 2)))
         deal_scales(nc, w1s_t, w1s_raw)
+        x_picked.append(keep.tile([P, S // 2], U32, name="x_picked1", tag="handed", align_bytes=64))
         nc.vector.tensor_copy(x_picked[1][:], x_all[:].bitcast(U32).indirect(entries(offs_t, S // 2, S // 2)))
         for t in range(PACK):
             for h in range(2):

@@ -3,7 +3,7 @@ from contextlib import ExitStack
 import concourse.mybir as mybir
 
 K, T, S, N, H, U = 512, 2048, 512, 512, 512, 1024
-FLOPS = 2 * K * N * S + 2 * H * N * U
+FLOPS = 2 * K * H * S + 2 * H * N * U
 
 F32 = mybir.dt.float32
 BF16 = mybir.dt.bfloat16
@@ -19,27 +19,46 @@ MULT = mybir.AluOpType.mult
 
 P = 128
 PACK = 4
-BANK = 512
+QUADRANTS = 4
 LIST = 16
-CHUNKS = ((0, 128, 0), (128, 384, 128), (512, 384, 384), (896, 128, 128))
+HALF = S // 2
+SPANS_A_BANK = 128
+BANKS = 8
+
+WIDTHS = (128, 384, 384, 128)
+LEFT_BY_SCALAR = (0, 192, 384, 128)
+STARTS = tuple(sum(WIDTHS[:n]) for n in range(len(WIDTHS)))
+LAST = len(WIDTHS) - 1
 
 
 def load_scale_rows(queues, tile, rows):
-    for q in range(4):
+    for q in range(QUADRANTS):
         queues[q].dma_start(out=tile[32 * q : 32 * q + 4, :].bitcast(I32), in_=rows[0, 4 * q : 4 * q + 4, :].bitcast(I32))
 
 
-def deal_words(nc, words, raw):
+def deal_words(nc, dealt, raw):
     nc.vector.tensor_copy(
-        out=words[:].rearrange("p (t m b) -> p t m b", t=PACK, b=2),
+        out=dealt[:].rearrange("p (t m b) -> p t m b", t=PACK, b=2),
         in_=raw[:].rearrange("p (m t b) -> p t m b", t=PACK, b=2),
     )
 
 
-def deal_scales(nc, scales, raw):
+def deal_scales(nc, dealt, raw):
     nc.vector.tensor_copy(
-        out=scales[:].rearrange("p (t m) -> p t m", t=PACK),
+        out=dealt[:].rearrange("p (t m) -> p t m", t=PACK),
         in_=raw[:].rearrange("p (m t) -> p t m", t=PACK),
+    )
+
+
+def product(nc, out, t, w_words, w_scales, codes, scales):
+    nc.tensor.matmul_mx(
+        out=out,
+        lhsT=w_words[:, 2 * P * t : 2 * P * (t + 1)].bitcast(FP4X4),
+        lhsT_scale=w_scales[:, P * t : P * (t + 1)],
+        rhs=codes.bitcast(FP8X4),
+        rhs_scale=scales,
+        start=True,
+        stop=True,
     )
 
 
@@ -47,12 +66,12 @@ def entries(tile, first, count):
     return tile[:, first // LIST : (first + count) // LIST]
 
 
-def planes_view(ap):
-    return ap.rearrange("p t (c i) -> p c t i", i=2)
+def planes_view(planes):
+    return planes.rearrange("p t (c i) -> p c t i", i=2)
 
 
-def packed_view(ap):
-    return ap.rearrange("p (c i) t -> p c t i", i=2)
+def interleaved_view(interleaved):
+    return interleaved.rearrange("p (c i) t -> p c t i", i=2)
 
 
 def tile_picked_ybrdgep_sag_po_kernel(
@@ -69,8 +88,8 @@ def tile_picked_ybrdgep_sag_po_kernel(
         rig_t = keep.tile([P, U // LIST], U16, name="rig_t")
         x_all = keep.tile([P, T], I32, name="x_all", align_bytes=64)
         xs_all = keep.tile([P, T], U8, name="xs_all", align_bytes=64)
-        w1_raw = keep.tile([P, 2 * N], U8, name="w1_raw", align_bytes=64)
-        w1s_raw = keep.tile([P, N], U8, name="w1s_raw", tag="handed", align_bytes=64)
+        w1_raw = keep.tile([P, 2 * H], U8, name="w1_raw", align_bytes=64)
+        w1s_raw = keep.tile([P, H], U8, name="w1s_raw", tag="w1s_then_x", align_bytes=64)
         w3_raw = keep.tile([P, 2 * N], U8, name="w3_raw", align_bytes=64)
         w3s_raw = keep.tile([P, N], U8, name="w3s_raw", align_bytes=64)
         unit_t = keep.tile([P, PACK], F32, name="unit_t")
@@ -86,148 +105,137 @@ def tile_picked_ybrdgep_sag_po_kernel(
         nc.sync.dma_start(out=x_all[:], in_=x_flat)
         nc.sync.dma_start(out=unit_t[:], in_=unit.rearrange("(p t) o -> p (t o)", t=PACK))
         nc.sync.dma_start(mid_t[:], mid)
-        load_scale_rows((nc.sync,) * 4, w1s_raw, w1_scales)
+        load_scale_rows((nc.sync,) * QUADRANTS, w1s_raw, w1_scales)
         nc.sync.dma_start(out=w3_raw[:].bitcast(I32), in_=w3_words[0].bitcast(I32))
         nc.sync.dma_start(rig_t[:], rig)
         nc.sync.dma_start(lef_t[:], lef)
-        load_scale_rows((nc.sync,) * 4, w3s_raw, w3_scales)
+        load_scale_rows((nc.sync,) * QUADRANTS, w3s_raw, w3_scales)
 
-        w1_t = keep.tile([P, 2 * N], U8, name="w1_t", align_bytes=64)
-        w1s_t = keep.tile([P, N], U8, name="w1s_t", align_bytes=64)
-        w3_t = keep.tile([P, 2 * N], U8, name="w3_t", align_bytes=64)
-        w3s_t = keep.tile([P, N], U8, name="w3s_t", align_bytes=64)
+        w1_dealt = keep.tile([P, 2 * H], U8, name="w1_dealt", align_bytes=64)
+        w1s_dealt = keep.tile([P, H], U8, name="w1s_dealt", align_bytes=64)
+        w3_dealt = keep.tile([P, 2 * N], U8, name="w3_dealt", align_bytes=64)
+        w3s_dealt = keep.tile([P, N], U8, name="w3s_dealt", align_bytes=64)
 
-        half = keep.tile([P, PACK], F32, name="half")
-        nc.scalar.activation(half[:], unit_t[:], COPY, scale=-0.5)
+        factor = keep.tile([P, PACK], F32, name="factor")
+        nc.scalar.activation(factor[:], unit_t[:], COPY, scale=-0.5)
 
         xs_picked = keep.tile([P, S], U8, name="xs_picked", align_bytes=64)
         nc.vector.tensor_copy(xs_picked[:], xs_all[:].indirect(offs_t[:]))
-        deal_words(nc, w1_t, w1_raw)
-        windows = [keep.tile([P, S], F32, name="window%d" % t, align_bytes=64) for t in range(PACK)]
-        x_picked = [keep.tile([P, S // 2], U32, name="x_picked0", align_bytes=64)]
-        nc.vector.tensor_copy(x_picked[0][:], x_all[:].bitcast(U32).indirect(entries(offs_t, 0, S // 2)))
-        deal_scales(nc, w1s_t, w1s_raw)
-        x_picked.append(keep.tile([P, S // 2], U32, name="x_picked1", tag="handed", align_bytes=64))
-        nc.vector.tensor_copy(x_picked[1][:], x_all[:].bitcast(U32).indirect(entries(offs_t, S // 2, S // 2)))
-        for t in range(PACK):
-            for h in range(2):
-                acc = psum.tile([P, S // 2], F32, name="bank%d" % (2 * t + h))
-                nc.tensor.matmul_mx(
-                    out=acc[:],
-                    lhsT=w1_t[:, 2 * P * t : 2 * P * (t + 1)].bitcast(FP4X4),
-                    lhsT_scale=w1s_t[:, P * t : P * (t + 1)],
-                    rhs=x_picked[h][:].bitcast(FP8X4),
-                    rhs_scale=xs_picked[:, h * S // 2 : (h + 1) * S // 2],
-                    start=True,
-                    stop=True,
-                )
-                columns = windows[t][:, h * S // 2 : (h + 1) * S // 2]
-                if t % 2 == 0:
-                    nc.scalar.activation(columns, acc[:], COPY, scale=half[:, t : t + 1])
-                else:
-                    nc.vector.tensor_scalar(columns, acc[:], half[:, t : t + 1], None, MULT)
-        deal_words(nc, w3_t, w3_raw)
-        deal_scales(nc, w3s_t, w3s_raw)
+        deal_words(nc, w1_dealt, w1_raw)
+        z = [keep.tile([P, S], F32, name="z%d" % t, align_bytes=64) for t in range(PACK)]
+        x_first = keep.tile([P, HALF], U32, name="x_first", align_bytes=64)
+        nc.vector.tensor_copy(x_first[:], x_all[:].bitcast(U32).indirect(entries(offs_t, 0, HALF)))
+        deal_scales(nc, w1s_dealt, w1s_raw)
+        x_second = keep.tile([P, HALF], U32, name="x_second", tag="w1s_then_x", align_bytes=64)
+        nc.vector.tensor_copy(x_second[:], x_all[:].bitcast(U32).indirect(entries(offs_t, HALF, HALF)))
 
-        out_rows = out_0.rearrange("(p t) r -> p t r", t=PACK)
+        for t in range(PACK):
+            for h, x_picked in enumerate((x_first, x_second)):
+                piers = slice(h * HALF, (h + 1) * HALF)
+                y = psum.tile([P, HALF], F32, name="y", tag="bank%d" % (2 * t + h))
+                product(nc, y[:], t, w1_dealt, w1s_dealt, x_picked[:], xs_picked[:, piers])
+                if t % 2 == 0:
+                    nc.scalar.activation(z[t][:, piers], y[:], COPY, scale=factor[:, t : t + 1])
+                else:
+                    nc.vector.tensor_scalar(z[t][:, piers], y[:], factor[:, t : t + 1], None, MULT)
+        deal_words(nc, w3_dealt, w3_raw)
+        deal_scales(nc, w3s_dealt, w3s_raw)
+
+        out_planes = out_0.rearrange("(p t) r -> p t r", t=PACK)
         out_words = out_1[0].rearrange("p n t -> p (n t)").bitcast(I32)
         out_scales = keep.tile([P, U], U8, name="out_scales", align_bytes=64)
 
         def look_up(n):
-            r0, width, shared = CHUNKS[n]
-            middle = keep.tile([P, PACK, width], F32, name="stage%d" % (n % 2), align_bytes=64)
-            left = keep.tile([P, PACK, shared], F32, name="left%d" % n, align_bytes=64) if shared else None
+            start, width, by_scalar = STARTS[n], WIDTHS[n], LEFT_BY_SCALAR[n]
+            by_vector = width - by_scalar
+            left, whole = None, None
+            middle = keep.tile([P, PACK, width], F32, name="middle", tag="middle_then_hid%d" % (n % 2), align_bytes=64)
+            if by_scalar:
+                left = keep.tile([P, PACK, by_scalar], F32, name="left", tag="left_then_codes%d" % (n % 2), align_bytes=64)
             part = keep.tile([P, PACK, width], F32, name="part%d" % n, align_bytes=64)
             for t in range(PACK):
-                nc.scalar.activation(middle[:, t, :], windows[t][:].indirect(entries(mid_t, r0, width)), COPY, scale=-2.0)
-                nc.vector.tensor_tensor(part[:, t, :], windows[t][:].indirect(entries(rig_t, r0, width)), middle[:, t, :], ADD)
-            for t in range(PACK if shared else 0):
-                nc.scalar.activation(left[:, t, :], windows[t][:].indirect(entries(lef_t, r0, shared)), COPY)
-            hid = keep.tile([P, width, PACK], BF16, name="stage%d" % (n % 2), align_bytes=64)
-            rest = width - shared
-            if rest:
-                whole = keep.tile([P, PACK, rest], F32, name="whole%d" % n, align_bytes=64)
+                nc.scalar.activation(middle[:, t, :], z[t][:].indirect(entries(mid_t, start, width)), COPY, scale=-2.0)
+                nc.vector.tensor_tensor(part[:, t, :], z[t][:].indirect(entries(rig_t, start, width)), middle[:, t, :], ADD)
+            if by_scalar:
                 for t in range(PACK):
-                    nc.vector.tensor_tensor(
-                        whole[:, t, :], windows[t][:].indirect(entries(lef_t, r0 + shared, rest)), part[:, t, shared:], ADD
-                    )
-            else:
-                whole = None
+                    nc.scalar.activation(left[:, t, :], z[t][:].indirect(entries(lef_t, start, by_scalar)), COPY)
+            hid = keep.tile([P, width, PACK], BF16, name="hid", tag="middle_then_hid%d" % (n % 2), align_bytes=64)
+            if by_vector:
+                whole = keep.tile([P, PACK, by_vector], F32, name="whole%d" % n, align_bytes=64)
+                for t in range(PACK):
+                    looked_up = z[t][:].indirect(entries(lef_t, start + by_scalar, by_vector))
+                    nc.vector.tensor_tensor(whole[:, t, :], looked_up, part[:, t, by_scalar:], ADD)
             return hid, part, left, whole
 
-        def round_rest(n, hid, part, left, whole):
-            r0, width, shared = CHUNKS[n]
-            if shared < width:
-                nc.vector.tensor_copy(out=packed_view(hid[:, shared:, :]), in_=planes_view(whole[:]))
+        def round_whole(n, hid, whole):
+            if whole is not None:
+                nc.vector.tensor_copy(out=interleaved_view(hid[:, LEFT_BY_SCALAR[n] :, :]), in_=planes_view(whole[:]))
 
-        def multiply(n, hid, part, left, whole):
-            r0, width, shared = CHUNKS[n]
-            if shared:
-                nc.vector.tensor_tensor(packed_view(hid[:, :shared, :]), planes_view(part[:, :, :shared]), planes_view(left[:]), ADD)
-            codes = keep.tile([P, width], U32, name="hid_codes%d" % n, align_bytes=64)
+        def multiply(n, hid, part, left):
+            start, width, by_scalar = STARTS[n], WIDTHS[n], LEFT_BY_SCALAR[n]
+            if left is not None:
+                nc.vector.tensor_tensor(
+                    interleaved_view(hid[:, :by_scalar, :]), planes_view(part[:, :, :by_scalar]), planes_view(left[:]), ADD
+                )
+            codes = keep.tile([P, width], U32, name="hid_codes", tag="left_then_codes%d" % (n % 2), align_bytes=64)
             scales = keep.tile([P, width], U8, name="hid_scales%d" % n, align_bytes=64)
             nc.vector.quantize_mx(out=codes[:].bitcast(FP8X4), scales=scales[:], in_=hid[:].rearrange("p r t -> p (r t)"))
             banks = []
-            last = n == len(CHUNKS) - 1
-            for block in range(width // P):
-                for first, count in ((0, 2), (2, 2)) if last else ((0, PACK),):
-                    acc = psum.tile([P, count, P], F32, name="bank%d" % ((r0 // P + block + first // 2) % 8))
-                    for t in range(first, first + count):
-                        nc.tensor.matmul_mx(
-                            out=acc[:, t - first, :],
-                            lhsT=w3_t[:, 2 * P * t : 2 * P * (t + 1)].bitcast(FP4X4),
-                            lhsT_scale=w3s_t[:, P * t : P * (t + 1)],
-                            rhs=codes[:, P * block : P * (block + 1)].bitcast(FP8X4),
-                            rhs_scale=scales[:, P * block : P * (block + 1)],
-                            start=True,
-                            stop=True,
-                        )
-                    banks.append(acc)
+            for g in range(width // SPANS_A_BANK):
+                columns = slice(SPANS_A_BANK * g, SPANS_A_BANK * (g + 1))
+                first_bank = start // SPANS_A_BANK + g
+                for b, held in enumerate(((0, 1), (2, 3)) if n == LAST else ((0, 1, 2, 3),)):
+                    bank = psum.tile([P, len(held), SPANS_A_BANK], F32, name="sums", tag="bank%d" % ((first_bank + b) % BANKS))
+                    for row, t in enumerate(held):
+                        product(nc, bank[:, row, :], t, w3_dealt, w3s_dealt, codes[:, columns], scales[:, columns])
+                    banks.append(bank)
             return banks
 
         def take_out(n, banks):
-            r0, width, shared = CHUNKS[n]
-            result = keep.tile([P, PACK, width], F32, name="result%d" % n, align_bytes=64)
-            if n == len(CHUNKS) - 1:
-                nc.scalar.copy(result[:, 0:2, :], banks[0][:])
-                nc.vector.tensor_copy(result[:, 2:4, :], banks[1][:])
-                nc.sync.dma_start(out=out_rows[:, :, r0 : r0 + width], in_=result[:])
-            else:
-                for block, acc in enumerate(banks):
-                    columns = result[:, :, P * block : P * (block + 1)]
-                    nc.scalar.copy(columns, acc[:])
-                    nc.sync.dma_start(out=out_rows[:, :, r0 + P * block : r0 + P * (block + 1)], in_=columns)
-            return result
+            results = []
+            for g in range(WIDTHS[n] // SPANS_A_BANK):
+                spans = slice(STARTS[n] + SPANS_A_BANK * g, STARTS[n] + SPANS_A_BANK * (g + 1))
+                result = keep.tile([P, PACK, SPANS_A_BANK], F32, name="result%d" % spans.start, align_bytes=64)
+                if n == LAST:
+                    nc.scalar.copy(result[:, 0:2, :], banks[0][:])
+                    nc.vector.tensor_copy(result[:, 2:4, :], banks[1][:])
+                else:
+                    nc.scalar.copy(result[:], banks[g][:])
+                nc.sync.dma_start(out=out_planes[:, :, spans], in_=result[:])
+                results.append(result)
+            return results
 
-        def round_out(n, result):
-            r0, width, shared = CHUNKS[n]
-            rounded = keep.tile([P, width, PACK], BF16, name="rounded%d" % n, align_bytes=64)
-            nc.vector.tensor_copy(out=packed_view(rounded[:]), in_=planes_view(result[:]))
+        def round_out(n, results):
+            rounded = keep.tile([P, WIDTHS[n], PACK], BF16, name="rounded%d" % n, align_bytes=64)
+            for g, result in enumerate(results):
+                columns = slice(SPANS_A_BANK * g, SPANS_A_BANK * (g + 1))
+                nc.vector.tensor_copy(out=interleaved_view(rounded[:, columns, :]), in_=planes_view(result[:]))
             return rounded
 
         def hand_on(n, rounded):
-            r0, width, shared = CHUNKS[n]
-            codes = keep.tile([P, width], I32, name="out_codes%d" % n, align_bytes=64)
+            spans = slice(STARTS[n], STARTS[n] + WIDTHS[n])
+            out_codes = keep.tile([P, WIDTHS[n]], I32, name="out_codes%d" % n, align_bytes=64)
             nc.vector.quantize_mx(
-                out=codes[:].bitcast(FP8X4), scales=out_scales[:, r0 : r0 + width], in_=rounded[:].rearrange("p r t -> p (r t)")
+                out=out_codes[:].bitcast(FP8X4), scales=out_scales[:, spans], in_=rounded[:].rearrange("p r t -> p (r t)")
             )
-            queue = nc.scalar if n == len(CHUNKS) - 1 else nc.sync
-            queue.dma_start(out=out_words[:, r0 : r0 + width], in_=codes[:])
+            queue = nc.scalar if n == LAST else nc.sync
+            queue.dma_start(out=out_words[:, spans], in_=out_codes[:])
 
-        banks, results = {}, {}
-        for n in range(len(CHUNKS) + 2):
-            if n < len(CHUNKS):
-                staged = look_up(n)
-            if 0 <= n - 1 < len(CHUNKS):
-                results[n - 1] = take_out(n - 1, banks[n - 1])
-            if 0 <= n - 2:
-                rounded = round_out(n - 2, results[n - 2])
-            if n < len(CHUNKS):
-                round_rest(n, *staged)
-            if 0 <= n - 2:
+        banks_of, results_of = {}, {}
+        for n in range(LAST + 3):
+            if n <= LAST:
+                hid, part, left, whole = look_up(n)
+            if 1 <= n <= LAST + 1:
+                results_of[n - 1] = take_out(n - 1, banks_of[n - 1])
+            if n >= 2:
+                rounded = round_out(n - 2, results_of[n - 2])
+            if n <= LAST:
+                round_whole(n, hid, whole)
+            if n >= 2:
                 hand_on(n - 2, rounded)
-            if n < len(CHUNKS):
-                banks[n] = multiply(n, *staged)
-        for q in range(4):
+            if n <= LAST:
+                banks_of[n] = multiply(n, hid, part, left)
+
+        for q in range(QUADRANTS):
             queue = nc.sync if q % 2 == 0 else nc.scalar
             queue.dma_start(out=out_2[0, 4 * q : 4 * q + 4, :].bitcast(I32), in_=out_scales[32 * q : 32 * q + 4, :].bitcast(I32))

from contextlib import ExitStack

import concourse.mybir as mybir

K, T, S, N, H, U = 512, 2048, 512, 512, 512, 1024
FLOPS = 2 * K * H * S + 2 * H * N * U

F32 = mybir.dt.float32
BF16 = mybir.dt.bfloat16
I32 = mybir.dt.int32
U32 = mybir.dt.uint32
U16 = mybir.dt.uint16
U8 = mybir.dt.uint8
FP8X4 = mybir.dt.float8_e4m3fn_x4
FP4X4 = mybir.dt.float4_e2m1fn_x4
COPY = mybir.ActivationFunctionType.Copy
ADD = mybir.AluOpType.add
MULT = mybir.AluOpType.mult

P = 128
PACK = 4
QUADRANTS = 4
LIST = 16
HALF = S // 2
SPANS_A_BANK = 128
BANKS = 8

WIDTHS = (128, 384, 384, 128)
LEFT_BY_SCALAR = (0, 192, 384, 128)
STARTS = tuple(sum(WIDTHS[:n]) for n in range(len(WIDTHS)))
LAST = len(WIDTHS) - 1


def load_scale_rows(queues, tile, rows):
    for q in range(QUADRANTS):
        queues[q].dma_start(out=tile[32 * q : 32 * q + 4, :].bitcast(I32), in_=rows[0, 4 * q : 4 * q + 4, :].bitcast(I32))


def deal_words(nc, dealt, raw):
    nc.vector.tensor_copy(
        out=dealt[:].rearrange("p (t m b) -> p t m b", t=PACK, b=2),
        in_=raw[:].rearrange("p (m t b) -> p t m b", t=PACK, b=2),
    )


def deal_scales(nc, dealt, raw):
    nc.vector.tensor_copy(
        out=dealt[:].rearrange("p (t m) -> p t m", t=PACK),
        in_=raw[:].rearrange("p (m t) -> p t m", t=PACK),
    )


def product(nc, out, t, w_words, w_scales, codes, scales):
    nc.tensor.matmul_mx(
        out=out,
        lhsT=w_words[:, 2 * P * t : 2 * P * (t + 1)].bitcast(FP4X4),
        lhsT_scale=w_scales[:, P * t : P * (t + 1)],
        rhs=codes.bitcast(FP8X4),
        rhs_scale=scales,
        start=True,
        stop=True,
    )


def entries(tile, first, count):
    return tile[:, first // LIST : (first + count) // LIST]


def planes_view(planes):
    return planes.rearrange("p t (c i) -> p c t i", i=2)


def interleaved_view(interleaved):
    return interleaved.rearrange("p (c i) t -> p c t i", i=2)


def tile_picked_ybrdgep_sag_po_kernel(
    tc, x_words, x_scales, w1_words, w1_scales, unit, w3_words, w3_scales, offs, lef, rig, mid, out_0, out_1, out_2
):
    nc = tc.nc
    with ExitStack() as ctx:
        keep = ctx.enter_context(tc.tile_pool(name="keep", bufs=1))
        psum = ctx.enter_context(tc.psum_pool(name="psum", bufs=1))

        offs_t = keep.tile([P, S // LIST], U16, name="offs_t")
        mid_t = keep.tile([P, U // LIST], U16, name="mid_t")
        lef_t = keep.tile([P, U // LIST], U16, name="lef_t")
        rig_t = keep.tile([P, U // LIST], U16, name="rig_t")
        x_all = keep.tile([P, T], I32, name="x_all", align_bytes=64)
        xs_all = keep.tile([P, T], U8, name="xs_all", align_bytes=64)
        w1_raw = keep.tile([P, 2 * H], U8, name="w1_raw", align_bytes=64)
        w1s_raw = keep.tile([P, H], U8, name="w1s_raw", tag="w1s_then_x", align_bytes=64)
        w3_raw = keep.tile([P, 2 * N], U8, name="w3_raw", align_bytes=64)
        w3s_raw = keep.tile([P, N], U8, name="w3s_raw", align_bytes=64)
        unit_t = keep.tile([P, PACK], F32, name="unit_t")

        nc.vector.memset(xs_all[:].bitcast(I32), 0)
        nc.vector.memset(w1s_raw[:].bitcast(I32), 0)
        nc.vector.memset(w3s_raw[:].bitcast(I32), 0)

        x_flat = x_words[0].rearrange("p n t -> p (n t)").bitcast(I32)
        nc.sync.dma_start(offs_t[:], offs)
        nc.sync.dma_start(out=w1_raw[:].bitcast(I32), in_=w1_words[0].bitcast(I32))
        load_scale_rows((nc.sync, nc.scalar, nc.sync, nc.scalar), xs_all, x_scales)
        nc.sync.dma_start(out=x_all[:], in_=x_flat)
        nc.sync.dma_start(out=unit_t[:], in_=unit.rearrange("(p t) o -> p (t o)", t=PACK))
        nc.sync.dma_start(mid_t[:], mid)
        load_scale_rows((nc.sync,) * QUADRANTS, w1s_raw, w1_scales)
        nc.sync.dma_start(out=w3_raw[:].bitcast(I32), in_=w3_words[0].bitcast(I32))
        nc.sync.dma_start(rig_t[:], rig)
        nc.sync.dma_start(lef_t[:], lef)
        load_scale_rows((nc.sync,) * QUADRANTS, w3s_raw, w3_scales)

        w1_dealt = keep.tile([P, 2 * H], U8, name="w1_dealt", align_bytes=64)
        w1s_dealt = keep.tile([P, H], U8, name="w1s_dealt", align_bytes=64)
        w3_dealt = keep.tile([P, 2 * N], U8, name="w3_dealt", align_bytes=64)
        w3s_dealt = keep.tile([P, N], U8, name="w3s_dealt", align_bytes=64)

        factor = keep.tile([P, PACK], F32, name="factor")
        nc.scalar.activation(factor[:], unit_t[:], COPY, scale=-0.5)

        xs_picked = keep.tile([P, S], U8, name="xs_picked", align_bytes=64)
        nc.vector.tensor_copy(xs_picked[:], xs_all[:].indirect(offs_t[:]))
        deal_words(nc, w1_dealt, w1_raw)
        z = [keep.tile([P, S], F32, name="z%d" % t, align_bytes=64) for t in range(PACK)]
        x_first = keep.tile([P, HALF], U32, name="x_first", align_bytes=64)
        nc.vector.tensor_copy(x_first[:], x_all[:].bitcast(U32).indirect(entries(offs_t, 0, HALF)))
        deal_scales(nc, w1s_dealt, w1s_raw)
        x_second = keep.tile([P, HALF], U32, name="x_second", tag="w1s_then_x", align_bytes=64)
        nc.vector.tensor_copy(x_second[:], x_all[:].bitcast(U32).indirect(entries(offs_t, HALF, HALF)))

        for t in range(PACK):
            for h, x_picked in enumerate((x_first, x_second)):
                piers = slice(h * HALF, (h + 1) * HALF)
                y = psum.tile([P, HALF], F32, name="y", tag="bank%d" % (2 * t + h))
                product(nc, y[:], t, w1_dealt, w1s_dealt, x_picked[:], xs_picked[:, piers])
                if t % 2 == 0:
                    nc.scalar.activation(z[t][:, piers], y[:], COPY, scale=factor[:, t : t + 1])
                else:
                    nc.vector.tensor_scalar(z[t][:, piers], y[:], factor[:, t : t + 1], None, MULT)
        deal_words(nc, w3_dealt, w3_raw)
        deal_scales(nc, w3s_dealt, w3s_raw)

        out_planes = out_0.rearrange("(p t) r -> p t r", t=PACK)
        out_words = out_1[0].rearrange("p n t -> p (n t)").bitcast(I32)
        out_scales = keep.tile([P, U], U8, name="out_scales", align_bytes=64)

        def look_up(n):
            start, width, by_scalar = STARTS[n], WIDTHS[n], LEFT_BY_SCALAR[n]
            by_vector = width - by_scalar
            left, whole = None, None
            middle = keep.tile([P, PACK, width], F32, name="middle", tag="middle_then_hid%d" % (n % 2), align_bytes=64)
            if by_scalar:
                left = keep.tile([P, PACK, by_scalar], F32, name="left", tag="left_then_codes%d" % (n % 2), align_bytes=64)
            part = keep.tile([P, PACK, width], F32, name="part%d" % n, align_bytes=64)
            for t in range(PACK):
                nc.scalar.activation(middle[:, t, :], z[t][:].indirect(entries(mid_t, start, width)), COPY, scale=-2.0)
                nc.vector.tensor_tensor(part[:, t, :], z[t][:].indirect(entries(rig_t, start, width)), middle[:, t, :], ADD)
            if by_scalar:
                for t in range(PACK):
                    nc.scalar.activation(left[:, t, :], z[t][:].indirect(entries(lef_t, start, by_scalar)), COPY)
            hid = keep.tile([P, width, PACK], BF16, name="hid", tag="middle_then_hid%d" % (n % 2), align_bytes=64)
            if by_vector:
                whole = keep.tile([P, PACK, by_vector], F32, name="whole%d" % n, align_bytes=64)
                for t in range(PACK):
                    looked_up = z[t][:].indirect(entries(lef_t, start + by_scalar, by_vector))
                    nc.vector.tensor_tensor(whole[:, t, :], looked_up, part[:, t, by_scalar:], ADD)
            return hid, part, left, whole

        def round_whole(n, hid, whole):
            if whole is not None:
                nc.vector.tensor_copy(out=interleaved_view(hid[:, LEFT_BY_SCALAR[n] :, :]), in_=planes_view(whole[:]))

        def multiply(n, hid, part, left):
            start, width, by_scalar = STARTS[n], WIDTHS[n], LEFT_BY_SCALAR[n]
            if left is not None:
                nc.vector.tensor_tensor(
                    interleaved_view(hid[:, :by_scalar, :]), planes_view(part[:, :, :by_scalar]), planes_view(left[:]), ADD
                )
            codes = keep.tile([P, width], U32, name="hid_codes", tag="left_then_codes%d" % (n % 2), align_bytes=64)
            scales = keep.tile([P, width], U8, name="hid_scales%d" % n, align_bytes=64)
            nc.vector.quantize_mx(out=codes[:].bitcast(FP8X4), scales=scales[:], in_=hid[:].rearrange("p r t -> p (r t)"))
            banks = []
            for g in range(width // SPANS_A_BANK):
                columns = slice(SPANS_A_BANK * g, SPANS_A_BANK * (g + 1))
                first_bank = start // SPANS_A_BANK + g
                for b, held in enumerate(((0, 1), (2, 3)) if n == LAST else ((0, 1, 2, 3),)):
                    bank = psum.tile([P, len(held), SPANS_A_BANK], F32, name="sums", tag="bank%d" % ((first_bank + b) % BANKS))
                    for row, t in enumerate(held):
                        product(nc, bank[:, row, :], t, w3_dealt, w3s_dealt, codes[:, columns], scales[:, columns])
                    banks.append(bank)
            return banks

        def take_out(n, banks):
            results = []
            for g in range(WIDTHS[n] // SPANS_A_BANK):
                spans = slice(STARTS[n] + SPANS_A_BANK * g, STARTS[n] + SPANS_A_BANK * (g + 1))
                result = keep.tile([P, PACK, SPANS_A_BANK], F32, name="result%d" % spans.start, align_bytes=64)
                if n == LAST:
                    nc.scalar.copy(result[:, 0:2, :], banks[0][:])
                    nc.vector.tensor_copy(result[:, 2:4, :], banks[1][:])
                else:
                    nc.scalar.copy(result[:], banks[g][:])
                nc.sync.dma_start(out=out_planes[:, :, spans], in_=result[:])
                results.append(result)
            return results

        def round_out(n, results):
            rounded = keep.tile([P, WIDTHS[n], PACK], BF16, name="rounded%d" % n, align_bytes=64)
            for g, result in enumerate(results):
                columns = slice(SPANS_A_BANK * g, SPANS_A_BANK * (g + 1))
                nc.vector.tensor_copy(out=interleaved_view(rounded[:, columns, :]), in_=planes_view(result[:]))
            return rounded

        def hand_on(n, rounded):
            spans = slice(STARTS[n], STARTS[n] + WIDTHS[n])
            out_codes = keep.tile([P, WIDTHS[n]], I32, name="out_codes%d" % n, align_bytes=64)
            nc.vector.quantize_mx(
                out=out_codes[:].bitcast(FP8X4), scales=out_scales[:, spans], in_=rounded[:].rearrange("p r t -> p (r t)")
            )
            queue = nc.scalar if n == LAST else nc.sync
            queue.dma_start(out=out_words[:, spans], in_=out_codes[:])

        banks_of, results_of = {}, {}
        for n in range(LAST + 3):
            if n <= LAST:
                hid, part, left, whole = look_up(n)
            if 1 <= n <= LAST + 1:
                results_of[n - 1] = take_out(n - 1, banks_of[n - 1])
            if n >= 2:
                rounded = round_out(n - 2, results_of[n - 2])
            if n <= LAST:
                round_whole(n, hid, whole)
            if n >= 2:
                hand_on(n - 2, rounded)
            if n <= LAST:
                banks_of[n] = multiply(n, hid, part, left)

        for q in range(QUADRANTS):
            queue = nc.sync if q % 2 == 0 else nc.scalar
            queue.dma_start(out=out_2[0, 4 * q : 4 * q + 4, :].bitcast(I32), in_=out_scales[32 * q : 32 * q + 4, :].bitcast(I32))
